import numpy as np, ml_dtypes
CORES = [50,52,122,124]
N = 4
import mx_ref
NC, WT = 256, 2
LR = np.float32(2.0 ** -4)
BF = ml_dtypes.bfloat16
def cut(t, i, w=512):
    return t[:, w * i:w * i + w]
def tile(rs):
    return np.stack(rs, axis=2).reshape(128, -1).astype(BF)
def pick(b):
    s = np.zeros((128, 128, 4), np.float32)
    s[np.arange(128), np.arange(128), b] = 1.0
    return mx_ref.quantize(s.reshape(128, 512).astype(BF))
def pk(c, s, i=0):
    return (np.ascontiguousarray(c[:, 512 * i:512 * i + 512]), mx_ref.live(s[:, 128 * i:128 * i + 128]))
def inputs(rng, e, E):
    def f(*shape):
        v = (rng.standard_normal(shape, dtype=np.float32) * np.exp2(rng.integers(-2, 3, shape[:-1] + (1,)))).astype(BF)
        return mx_ref.spread((v.astype(np.float32) * np.exp2(rng.integers(-E, E + 1, shape[:-2] + (1, 1))).astype(np.float32)).astype(BF), rng, e)
    def packed(k):
        c = np.zeros((N, 128, k * 512), np.uint8); s = np.zeros((N, 128, k * 128), np.uint8)
        for r in range(N):
            for i in range(k):
                a, b = mx_ref.quantize(f(128, 512)); c[r][:, 512 * i:512 * i + 512] = a; s[r][:, 128 * i:128 * i + 128] = mx_ref.plane(b, rng)
        return c, s
    d = {}
    d["wc"], d["ws"] = packed(WT)
    d["gr"] = f(N, 128, WT * 512)
    d["x"] = f(N, 128, 4 * NC)
    return d
def setup_inputs(rng):
    return inputs(rng, 0, 0)
def setup_inputs_blocks(rng):
    return inputs(rng, 2, 0)
def setup_inputs_wide(rng):
    return inputs(rng, 0, 4)
def setup_inputs_faint(rng):
    d = setup_inputs(rng); d["gr"] = mx_ref.flush((d["gr"].astype(np.float32) * np.float32(2.0 ** -12)).astype(BF))
    return d
def reference(wc, ws, gr, x):
    S = [pick(t) for t in range(4)]
    H = [mx_ref.quantize(tile([mx_ref.matmul(S[t], pk(wc[j], ws[j], i)) - cut(gr[j], i).astype(np.float32)[:, t::4] * LR for t in range(4)])) for j in range(N) for i in range(WT)]
    y = np.zeros((N, 128, N * WT * NC), np.float32)
    for r in range(N):
        X = mx_ref.quantize(x[r])
        for b in range(N * WT):
            y[r][:, NC * b:NC * b + NC] = mx_ref.matmul(H[b], X)
    return {"y": y}

@@ -1,0 +1,192 @@
+from concourse.bass import DstId, RemoteDMATransfer
+from concourse.mybir import dt, AluOpType, ActivationFunctionType
+
+NR = 4
+WT = 2
+NC = 256
+TW = 128
+EL = 4 * TW
+BANK = 512
+LR = 2.0 ** -4
+
+SCRATCH = {
+    "one": ("sbuf", [128, EL + 4], "bfloat16"),
+    "band": ("sbuf", [128, EL + 4], "bfloat16"),
+    "sc": ("sbuf", [128, 4 * TW], "float8_e4m3fn_x4"),
+    "ss": ("sbuf", [128, 4 * TW], "uint8"),
+    "pc": ("sbuf", [128, WT * TW], "float8_e4m3fn_x4"),
+    "ps": ("sbuf", [128, WT * TW], "uint8"),
+    "gt": ("sbuf", [128, WT * EL], "bfloat16"),
+    "gs": ("sbuf", [128, WT * EL], "bfloat16"),
+    "xt": ("sbuf", [128, 4 * NC], "bfloat16"),
+    "xc": ("sbuf", [128, NC], "float8_e4m3fn_x4"),
+    "xs": ("sbuf", [128, NC], "uint8"),
+    "v": ("sbuf", [128, WT * EL], "bfloat16"),
+    "vc": ("sbuf", [128, WT * TW], "float8_e4m3fn_x4"),
+    "vs": ("sbuf", [128, WT * TW], "uint8"),
+    "yt": ("sbuf", [128, NR * WT * NC], "float32"),
+    "acc": ("psum", [128, 8 * BANK], "float32"),
+}
+for _j in range(NR):
+    SCRATCH["rc%d" % _j] = ("sbuf", [128, WT * TW], "float8_e4m3fn_x4")
+    SCRATCH["rs%d" % _j] = ("sbuf", [128, WT * TW], "uint8")
+
+SEMAPHORES = (["lg0", "lg1", "lwc", "lws", "lx", "ones", "sel", "sq", "g0", "g1", "tt0", "tt1", "vq", "xq", "sent", "sty", "stc"]
+              + ["d%d" % k for k in range(8)] + ["m%d" % k for k in range(8)] + ["c%d" % k for k in range(8)]
+              + ["ac%d" % j for j in range(NR)] + ["as%d" % j for j in range(NR)])
+
+
+def bits(mask):
+    return bin(mask).count("1")
+
+
+def relays(src, T, topo):
+    far = [d for d in T.cores if topo.chip(d) != topo.chip(src)]
+    if all(topo.may_write(src, d) for d in far):
+        return []
+    own = [c for c in range(topo.CHIPS * topo.CORES_PER_CHIP)
+           if topo.chip(c) == topo.chip(src) and T.rank_of(c) is None and all(topo.may_write(c, d) for d in far)]
+    own.sort(key=lambda c: (topo.die(c) != topo.die(src), c))
+    return list(zip(own, far))
+
+
+def send(g, core, T, topo, j, dests, mask, what, src):
+    land = T["r%s%d" % (what, j)]
+    if what == "c":
+        out, in_ = land[:].bitcast(dt.uint8), src[:].bitcast(dt.uint8)
+    else:
+        out, in_ = land[:], src[:]
+    ids = []
+    for d in dests:
+        rid, pid, _ = topo.addr(d)
+        ids.append(DstId(rid=rid, pnc=pid))
+    g.remote_dma_fused([RemoteDMATransfer(dst_ids=ids, dma_engine_mask=mask, remote_sem=T.sem["a%s%d" % (what, j)],
+                                          srcs=[in_], dsts=[out for _ in dests])], local_sem=T.sem.sent)
+    return bits(mask)
+
+
+def arrival_count(src, dst, T, topo):
+    if topo.chip(src) == topo.chip(dst):
+        return bits(near_mask(src, dst, T, topo))
+    rel = relays(src, T, topo)
+    for r, d in rel:
+        if d == dst:
+            return bits(topo.mask(r, dst))
+    return bits(topo.mask(src, dst))
+
+
+def near_mask(src, dst, T, topo):
+    m = topo.mask(src, dst)
+    if not relays(src, T, topo):
+        for d in T.cores:
+            if topo.chip(d) != topo.chip(src):
+                m &= ~topo.mask(src, d)
+    return m
+
+
+def relay_program(g, core, T, topo):
+    for src in T.cores:
+        for r, d in relays(src, T, topo):
+            if r == core:
+                j = T.rank_of(src)
+                n = bits(topo.mask(src, core))
+                sent = 0
+                for what in ("c", "s"):
+                    g.wait_ge(T.sem["a%s%d" % (what, j)], n)
+                    sent += send(g, core, T, topo, j, [d], topo.mask(core, d), what, T["r%s%d" % (what, j)])
+                g.wait_ge(T.sem.sent, sent)
+
+
+def rank_program(g, core, T, topo):
+    rank = T.rank_of(core)
+    if rank is None:
+        relay_program(g, core, T, topo)
+        return
+    S = T.sem
+    near = [d for d in T.cores if d != core and topo.chip(d) == topo.chip(core)]
+    far = [d for d in T.cores if topo.chip(d) != topo.chip(core)]
+    rel = relays(core, T, topo)
+    order = [core] + near + sorted(far, key=lambda c: len(relays(c, T, topo)))
+
+    g.sync.dma_start(T.gt[:, 0:EL], T.gr[:, 0:EL]).then_inc(S.lg0, 16)
+    g.scalar.dma_start(T.pc[:].bitcast(dt.uint8), T.wc[:]).then_inc(S.lwc, 16)
+    g.sync.dma_start(T.ps[:], T.ws[:]).then_inc(S.lws, 16)
+    g.scalar.dma_start(T.gt[:, EL:2 * EL], T.gr[:, EL:2 * EL]).then_inc(S.lg1, 16)
+    g.sync.dma_start(T.xt[:], T.x[:]).then_inc(S.lx, 16)
+
+    g.vector.memset(T.one[:], 1.0).then_inc(S.ones, 1)
+    g.wait_ge(S.ones, 1)
+    g.affine_select(T.band[:], T.one[:], [[-1, EL + 4]], AluOpType.is_equal, 0.0, 3, 4).then_inc(S.sel, 1)
+    g.vector.wait_ge(S.sel, 1)
+    for b in range(4):
+        g.vector.quantize_mx(T.sc[:, TW * b:TW * b + TW], T.ss[:, TW * b:TW * b + TW],
+                             T.band[:, 3 - b:3 - b + EL]).then_inc(S.sq, 1)
+
+    g.tensor.wait_ge(S.sq, 4)
+    g.tensor.wait_ge(S.lwc, 16)
+    g.tensor.wait_ge(S.lws, 16)
+    for i in range(WT):
+        for b in range(4):
+            k = 4 * i + b
+            g.tensor.matmul_mx(T.acc[:, BANK * k:BANK * k + TW], T.sc[:, TW * b:TW * b + TW], T.ss[:, TW * b:TW * b + TW],
+                               T.pc[:, TW * i:TW * i + TW], T.ps[:, TW * i:TW * i + TW], True, True).then_inc(S["d%d" % k], 1)
+
+    g.vector.wait_ge(S.lg0, 16)
+    g.vector.tensor_scalar(T.gs[:, 0:EL], T.gt[:, 0:EL], LR, None, AluOpType.mult).then_inc(S.g0, 1)
+    g.scalar.wait_ge(S.lg1, 16)
+    g.scalar.activation(T.gs[:, EL:2 * EL], T.gt[:, EL:2 * EL], ActivationFunctionType.Copy, scale=LR).then_inc(S.g1, 1)
+    for i in range(WT):
+        g.vector.wait_ge(S["g%d" % i], 1)
+        for b in range(4):
+            k = 4 * i + b
+            g.vector.wait_ge(S["d%d" % k], 1)
+            g.vector.tensor_tensor(T.v[:, EL * i + b:EL * (i + 1):4], T.acc[:, BANK * k:BANK * k + TW],
+                                   T.gs[:, EL * i + b:EL * (i + 1):4], AluOpType.subtract).then_inc(S["tt%d" % i], 1)
+        g.vector.wait_ge(S["tt%d" % i], 4)
+        g.vector.quantize_mx(T.vc[:, TW * i:TW * i + TW], T.vs[:, TW * i:TW * i + TW],
+                             T.v[:, EL * i:EL * i + EL]).then_inc(S.vq, 1)
+    g.vector.wait_ge(S.lx, 16)
+    g.vector.quantize_mx(T.xc[:], T.xs[:], T.xt[:]).then_inc(S.xq, 1)
+
+    sent = 0
+    g.wait_ge(S.vq, WT)
+    if rel:
+        first, m = [r for r, _ in rel], topo.mask(core, rel[0][0])
+    else:
+        first, m = far, topo.mask(core, far[0])
+    for dests, mask in ((first, m), (near, near_mask(core, near[0], T, topo))):
+        sent += send(g, core, T, topo, rank, dests, mask, "c", T.vc)
+        sent += send(g, core, T, topo, rank, dests, mask, "s", T.vs)
+    g.wait_ge(S.sent, sent)
+
+    for k, src in enumerate(order):
+        j = T.rank_of(src)
+        if src == core:
+            g.tensor.wait_ge(S.xq, 1)
+            g.tensor.wait_ge(S.vq, WT)
+            cc, cs = T.vc, T.vs
+        else:
+            n = arrival_count(src, core, T, topo)
+            g.tensor.wait_ge(S["ac%d" % j], n)
+            g.tensor.wait_ge(S["as%d" % j], n)
+            cc, cs = T["rc%d" % j], T["rs%d" % j]
+        for i in range(WT):
+            q = 2 * k + i
+            g.tensor.matmul_mx(T.acc[:, BANK * q:BANK * q + NC], cc[:, TW * i:TW * i + TW], cs[:, TW * i:TW * i + TW],
+                               T.xc[:], T.xs[:], True, True).then_inc(S["m%d" % q], 1)
+        for i in range(WT):
+            q = 2 * k + i
+            a = NC * (2 * j + i)
+            out, acc, done = T.yt[:, a:a + NC], T.acc[:, BANK * q:BANK * q + NC], S["c%d" % q]
+            if i == 0:
+                g.vector.wait_ge(S["m%d" % q], 1)
+                g.vector.tensor_copy(out, acc).then_inc(done, 1)
+                dq, st = g.sync, S.sty
+            else:
+                g.scalar.wait_ge(S["m%d" % q], 1)
+                g.scalar.activation(out, acc, ActivationFunctionType.Copy).then_inc(done, 1)
+                dq, st = g.scalar, S.stc
+            dq.wait_ge(done, 1)
+            dq.dma_start(T.y[:, a:a + NC], out).then_inc(st, 16)
+    g.sync.wait_ge(S.sty, 16 * NR)
+    g.scalar.wait_ge(S.stc, 16 * NR)

@@ -10,7 +10,7 @@ BANK = 512
 LR = 2.0 ** -4
 
 SCRATCH = {
-    "one": ("sbuf", [128, EL + 4], "bfloat16"),
+    "ramp": ("sbuf", [128, TW], "float32"),
     "band": ("sbuf", [128, EL + 4], "bfloat16"),
     "sc": ("sbuf", [128, 4 * TW], "float8_e4m3fn_x4"),
     "ss": ("sbuf", [128, 4 * TW], "uint8"),
@@ -31,7 +31,8 @@ for _j in range(NR):
     SCRATCH["rc%d" % _j] = ("sbuf", [128, WT * TW], "float8_e4m3fn_x4")
     SCRATCH["rs%d" % _j] = ("sbuf", [128, WT * TW], "uint8")
 
-SEMAPHORES = (["lg0", "lg1", "lwc", "lws", "lx", "ones", "sel", "sq", "g0", "g1", "tt0", "tt1", "vq", "xq", "sent", "sty", "stc"]
+SEMAPHORES = (["lg0", "lg1", "lwc", "lws", "lx", "ramp", "zero", "ones", "sq", "g0", "g1", "tt0", "tt1", "vq0", "vq1", "xq",
+               "sent", "sty", "stc"]
               + ["d%d" % k for k in range(8)] + ["m%d" % k for k in range(8)] + ["c%d" % k for k in range(8)]
               + ["ac%d" % j for j in range(NR)] + ["as%d" % j for j in range(NR)])
 
@@ -40,22 +41,55 @@ def bits(mask):
     return bin(mask).count("1")
 
 
+def far_of(src, T, topo):
+    return [d for d in T.cores if topo.chip(d) != topo.chip(src)]
+
+
 def relays(src, T, topo):
-    far = [d for d in T.cores if topo.chip(d) != topo.chip(src)]
+    far = far_of(src, T, topo)
     if all(topo.may_write(src, d) for d in far):
-        return []
+        return [], None
     own = [c for c in range(topo.CHIPS * topo.CORES_PER_CHIP)
            if topo.chip(c) == topo.chip(src) and T.rank_of(c) is None and all(topo.may_write(c, d) for d in far)]
     own.sort(key=lambda c: (topo.die(c) != topo.die(src), c))
-    return list(zip(own, far))
+    return own[:len(far)], own[len(far)]
 
 
-def send(g, core, T, topo, j, dests, mask, what, src):
+def near_mask(src, dst, T, topo):
+    m = topo.mask(src, dst)
+    for d in far_of(src, T, topo):
+        if topo.may_write(src, d):
+            m &= ~topo.mask(src, d)
+    return m
+
+
+def calls(core, T, topo):
+    near = [d for d in T.cores if d != core and topo.chip(d) == topo.chip(core)]
+    far = far_of(core, T, topo)
+    nm, w = near_mask(core, near[0], T, topo), WT * TW
+    rc, rp = relays(core, T, topo)
+    if rc:
+        m = topo.mask(core, rc[0])
+        return [(1, rc, m, "c", 0, TW), (2, [rp], topo.mask(core, rp), "s", 0, w), (2, rc, m, "c", TW, w),
+                (2, near, nm, "c", 0, w), (2, near, nm, "s", 0, w)]
+    m = topo.mask(core, far[0])
+    return [(1, near, nm, "c", 0, TW), (2, far, m, "c", 0, w), (2, far, m, "s", 0, w),
+            (2, near, nm, "c", TW, w), (2, near, nm, "s", 0, w)]
+
+
+def arrivals(src, dst, what, T, topo):
+    rc, rp = relays(src, T, topo)
+    if rc and topo.chip(src) != topo.chip(dst):
+        return bits(topo.mask(rp if what == "s" else rc[far_of(src, T, topo).index(dst)], dst))
+    return sum(bits(m) for _, dests, m, w, _, _ in calls(src, T, topo) if w == what and dst in dests)
+
+
+def send(g, T, topo, j, dests, mask, what, src, a, b):
     land = T["r%s%d" % (what, j)]
     if what == "c":
-        out, in_ = land[:].bitcast(dt.uint8), src[:].bitcast(dt.uint8)
+        out, in_ = land[:, a:b].bitcast(dt.uint8), src[:, a:b].bitcast(dt.uint8)
     else:
-        out, in_ = land[:], src[:]
+        out, in_ = land[:, a:b], src[:, a:b]
     ids = []
     for d in dests:
         rid, pid, _ = topo.addr(d)
@@ -65,36 +99,16 @@ def send(g, core, T, topo, j, dests, mask, what, src):
     return bits(mask)
 
 
-def arrival_count(src, dst, T, topo):
-    if topo.chip(src) == topo.chip(dst):
-        return bits(near_mask(src, dst, T, topo))
-    rel = relays(src, T, topo)
-    for r, d in rel:
-        if d == dst:
-            return bits(topo.mask(r, dst))
-    return bits(topo.mask(src, dst))
-
-
-def near_mask(src, dst, T, topo):
-    m = topo.mask(src, dst)
-    if not relays(src, T, topo):
-        for d in T.cores:
-            if topo.chip(d) != topo.chip(src):
-                m &= ~topo.mask(src, d)
-    return m
-
-
 def relay_program(g, core, T, topo):
     for src in T.cores:
-        for r, d in relays(src, T, topo):
-            if r == core:
-                j = T.rank_of(src)
-                n = bits(topo.mask(src, core))
-                sent = 0
-                for what in ("c", "s"):
-                    g.wait_ge(T.sem["a%s%d" % (what, j)], n)
-                    sent += send(g, core, T, topo, j, [d], topo.mask(core, d), what, T["r%s%d" % (what, j)])
-                g.wait_ge(T.sem.sent, sent)
+        rc, rp = relays(src, T, topo)
+        if core in rc or core == rp:
+            far = far_of(src, T, topo)
+            what, dests = ("s", far) if core == rp else ("c", [far[rc.index(core)]])
+            j = T.rank_of(src)
+            g.wait_ge(T.sem["a%s%d" % (what, j)], arrivals(src, core, what, T, topo))
+            n = send(g, T, topo, j, dests, topo.mask(core, dests[0]), what, T["r%s%d" % (what, j)], 0, WT * TW)
+            g.wait_ge(T.sem.sent, n)
 
 
 def rank_program(g, core, T, topo):
@@ -104,9 +118,8 @@ def rank_program(g, core, T, topo):
         return
     S = T.sem
     near = [d for d in T.cores if d != core and topo.chip(d) == topo.chip(core)]
-    far = [d for d in T.cores if topo.chip(d) != topo.chip(core)]
-    rel = relays(core, T, topo)
-    order = [core] + near + sorted(far, key=lambda c: len(relays(c, T, topo)))
+    far = far_of(core, T, topo)
+    order = [core] + near + sorted(far, key=lambda c: len(relays(c, T, topo)[0]))
 
     g.sync.dma_start(T.gt[:, 0:EL], T.gr[:, 0:EL]).then_inc(S.lg0, 16)
     g.scalar.dma_start(T.pc[:].bitcast(dt.uint8), T.wc[:]).then_inc(S.lwc, 16)
@@ -114,10 +127,14 @@ def rank_program(g, core, T, topo):
     g.scalar.dma_start(T.gt[:, EL:2 * EL], T.gr[:, EL:2 * EL]).then_inc(S.lg1, 16)
     g.sync.dma_start(T.xt[:], T.x[:]).then_inc(S.lx, 16)
 
-    g.vector.memset(T.one[:], 1.0).then_inc(S.ones, 1)
-    g.wait_ge(S.ones, 1)
-    g.affine_select(T.band[:], T.one[:], [[-1, EL + 4]], AluOpType.is_equal, 0.0, 3, 4).then_inc(S.sel, 1)
-    g.vector.wait_ge(S.sel, 1)
+    g.vector.memset(T.band[:], 0.0).then_inc(S.zero, 1)
+    g.iota(T.ramp[:], [[-1, TW]], 3, 4, allow_small_or_imprecise_dtypes=True).then_inc(S.ramp, 1)
+    g.vector.wait_ge(S.zero, 1)
+    g.vector.wait_ge(S.ramp, 1)
+    for a in range(4):
+        g.vector.tensor_scalar(T.band[32 * a:32 * a + 32, TW * a:TW * a + TW], T.ramp[32 * a:32 * a + 32, :],
+                               float(TW * a), None, AluOpType.is_equal).then_inc(S.ones, 1)
+    g.vector.wait_ge(S.ones, 4)
     for b in range(4):
         g.vector.quantize_mx(T.sc[:, TW * b:TW * b + TW], T.ss[:, TW * b:TW * b + TW],
                              T.band[:, 3 - b:3 - b + EL]).then_inc(S.sq, 1)
@@ -144,31 +161,28 @@ def rank_program(g, core, T, topo):
                                    T.gs[:, EL * i + b:EL * (i + 1):4], AluOpType.subtract).then_inc(S["tt%d" % i], 1)
         g.vector.wait_ge(S["tt%d" % i], 4)
         g.vector.quantize_mx(T.vc[:, TW * i:TW * i + TW], T.vs[:, TW * i:TW * i + TW],
-                             T.v[:, EL * i:EL * i + EL]).then_inc(S.vq, 1)
+                             T.v[:, EL * i:EL * i + EL]).then_inc(S["vq%d" % i], 1)
     g.vector.wait_ge(S.lx, 16)
     g.vector.quantize_mx(T.xc[:], T.xs[:], T.xt[:]).then_inc(S.xq, 1)
 
-    sent = 0
-    g.wait_ge(S.vq, WT)
-    if rel:
-        first, m = [r for r, _ in rel], topo.mask(core, rel[0][0])
-    else:
-        first, m = far, topo.mask(core, far[0])
-    for dests, mask in ((first, m), (near, near_mask(core, near[0], T, topo))):
-        sent += send(g, core, T, topo, rank, dests, mask, "c", T.vc)
-        sent += send(g, core, T, topo, rank, dests, mask, "s", T.vs)
+    sent = made = 0
+    for tiles, dests, mask, what, a, b in calls(core, T, topo):
+        while made < tiles:
+            g.wait_ge(S["vq%d" % made], 1)
+            made += 1
+        sent += send(g, T, topo, rank, dests, mask, what, T["v" + what], a, b)
     g.wait_ge(S.sent, sent)
 
     for k, src in enumerate(order):
         j = T.rank_of(src)
         if src == core:
             g.tensor.wait_ge(S.xq, 1)
-            g.tensor.wait_ge(S.vq, WT)
+            for i in range(WT):
+                g.tensor.wait_ge(S["vq%d" % i], 1)
             cc, cs = T.vc, T.vs
         else:
-            n = arrival_count(src, core, T, topo)
-            g.tensor.wait_ge(S["ac%d" % j], n)
-            g.tensor.wait_ge(S["as%d" % j], n)
+            g.tensor.wait_ge(S["ac%d" % j], arrivals(src, core, "c", T, topo))
+            g.tensor.wait_ge(S["as%d" % j], arrivals(src, core, "s", T, topo))
             cc, cs = T["rc%d" % j], T["rs%d" % j]
         for i in range(WT):
             q = 2 * k + i

@@ -34,92 +34,101 @@ for _j in range(NR):
 SEMAPHORES = (["lg0", "lg1", "lwc", "lws", "lx", "ramp", "zero", "ones", "sq", "g0", "g1", "tt0", "tt1", "vq0", "vq1", "xq",
                "sent", "sty", "stc"]
               + ["d%d" % k for k in range(8)] + ["m%d" % k for k in range(8)] + ["c%d" % k for k in range(8)]
-              + ["ac%d" % j for j in range(NR)] + ["as%d" % j for j in range(NR)])
+              + ["a%s%d" % (w, j) for w in "tcs" for j in range(NR)])
 
 
 def bits(mask):
     return bin(mask).count("1")
 
 
-def far_of(src, T, topo):
-    return [d for d in T.cores if topo.chip(d) != topo.chip(src)]
+def plan(T, topo):
+    W = WT * TW
+    steps, passed = {}, []
+
+    def add(core, needs, j, kind, a, b, dests, mask):
+        steps.setdefault(core, []).append((needs, j, kind, a, b, dests, mask))
+
+    for j, src in enumerate(T.cores):
+        near = [d for d in T.cores if d != src and topo.chip(d) == topo.chip(src)]
+        far = [d for d in T.cores if topo.chip(d) != topo.chip(src)]
+        half, full = ["vq0"], ["vq0", "vq1"]
+        if all(topo.may_write(src, d) for d in far):
+            off = topo.mask(src, far[0])
+            inner = topo.mask(src, near[0]) & ~off
+            peer = [d for d in far if all(topo.may_write(d, s) for s in near)] or far
+            rest = [d for d in far if d not in peer]
+            add(src, half, j, "t", 0, TW, near, inner)
+            add(src, full, j, "s", 0, W, peer, off)
+            add(src, full, j, "c", 0, W, far, off)
+            add(src, full, j, "c", TW, W, near, inner)
+            add(src, full, j, "s", 0, W, near, inner)
+            if rest:
+                passed.append((peer[0], j, rest, topo.mask(peer[0], rest[0]) & ~topo.mask(peer[0], src)))
+        else:
+            own = [c for c in range(topo.CHIPS * topo.CORES_PER_CHIP)
+                   if topo.chip(c) == topo.chip(src) and T.rank_of(c) is None and all(topo.may_write(c, d) for d in far)]
+            own.sort(key=lambda c: (topo.die(c) != topo.die(src), c))
+            rc, rp = own[:len(far)], own[len(far)]
+            m, nm = topo.mask(src, rc[0]), topo.mask(src, near[0])
+            add(src, half, j, "t", 0, TW, rc, m)
+            add(src, full, j, "s", 0, W, [rp], topo.mask(src, rp))
+            add(src, full, j, "c", TW, W, rc, m)
+            add(src, full, j, "c", 0, W, near, nm)
+            add(src, full, j, "s", 0, W, near, nm)
+            for r, d in zip(rc, far):
+                add(r, ["at%d" % j], j, "t", 0, TW, [d], topo.mask(r, d))
+                add(r, ["ac%d" % j], j, "c", TW, W, [d], topo.mask(r, d))
+            add(rp, ["as%d" % j], j, "s", 0, W, far, topo.mask(rp, far[0]))
+    for c, j, dests, mask in passed:
+        add(c, ["as%d" % j], j, "s", 0, W, dests, mask)
+    return steps
 
 
-def relays(src, T, topo):
-    far = far_of(src, T, topo)
-    if all(topo.may_write(src, d) for d in far):
-        return [], None
-    own = [c for c in range(topo.CHIPS * topo.CORES_PER_CHIP)
-           if topo.chip(c) == topo.chip(src) and T.rank_of(c) is None and all(topo.may_write(c, d) for d in far)]
-    own.sort(key=lambda c: (topo.die(c) != topo.die(src), c))
-    return own[:len(far)], own[len(far)]
+def landed(steps, dst):
+    n = {}
+    for own in steps.values():
+        for _, j, kind, _, _, dests, mask in own:
+            if dst in dests:
+                name = "a%s%d" % (kind, j)
+                n[name] = n.get(name, 0) + bits(mask)
+    return n
 
 
-def near_mask(src, dst, T, topo):
-    m = topo.mask(src, dst)
-    for d in far_of(src, T, topo):
-        if topo.may_write(src, d):
-            m &= ~topo.mask(src, d)
-    return m
-
-
-def calls(core, T, topo):
-    near = [d for d in T.cores if d != core and topo.chip(d) == topo.chip(core)]
-    far = far_of(core, T, topo)
-    nm, w = near_mask(core, near[0], T, topo), WT * TW
-    rc, rp = relays(core, T, topo)
-    if rc:
-        m = topo.mask(core, rc[0])
-        return [(1, rc, m, "c", 0, TW), (2, [rp], topo.mask(core, rp), "s", 0, w), (2, rc, m, "c", TW, w),
-                (2, near, nm, "c", 0, w), (2, near, nm, "s", 0, w)]
-    m = topo.mask(core, far[0])
-    return [(1, near, nm, "c", 0, TW), (2, far, m, "c", 0, w), (2, far, m, "s", 0, w),
-            (2, near, nm, "c", TW, w), (2, near, nm, "s", 0, w)]
-
-
-def arrivals(src, dst, what, T, topo):
-    rc, rp = relays(src, T, topo)
-    if rc and topo.chip(src) != topo.chip(dst):
-        return bits(topo.mask(rp if what == "s" else rc[far_of(src, T, topo).index(dst)], dst))
-    return sum(bits(m) for _, dests, m, w, _, _ in calls(src, T, topo) if w == what and dst in dests)
-
-
-def send(g, T, topo, j, dests, mask, what, src, a, b):
-    land = T["r%s%d" % (what, j)]
-    if what == "c":
-        out, in_ = land[:, a:b].bitcast(dt.uint8), src[:, a:b].bitcast(dt.uint8)
-    else:
+def exchange(g, core, T, topo, steps):
+    count = landed(steps, core)
+    met, sent = [], 0
+    for needs, j, kind, a, b, dests, mask in steps.get(core, []):
+        for name in needs:
+            if name not in met:
+                g.wait_ge(T.sem[name], count.get(name, 1))
+                met.append(name)
+        codes = kind != "s"
+        land = T["r%s%d" % ("c" if codes else "s", j)]
+        src = land if T.rank_of(core) != j else (T.vc if codes else T.vs)
         out, in_ = land[:, a:b], src[:, a:b]
-    ids = []
-    for d in dests:
-        rid, pid, _ = topo.addr(d)
-        ids.append(DstId(rid=rid, pnc=pid))
-    g.remote_dma_fused([RemoteDMATransfer(dst_ids=ids, dma_engine_mask=mask, remote_sem=T.sem["a%s%d" % (what, j)],
-                                          srcs=[in_], dsts=[out for _ in dests])], local_sem=T.sem.sent)
-    return bits(mask)
-
-
-def relay_program(g, core, T, topo):
-    for src in T.cores:
-        rc, rp = relays(src, T, topo)
-        if core in rc or core == rp:
-            far = far_of(src, T, topo)
-            what, dests = ("s", far) if core == rp else ("c", [far[rc.index(core)]])
-            j = T.rank_of(src)
-            g.wait_ge(T.sem["a%s%d" % (what, j)], arrivals(src, core, what, T, topo))
-            n = send(g, T, topo, j, dests, topo.mask(core, dests[0]), what, T["r%s%d" % (what, j)], 0, WT * TW)
-            g.wait_ge(T.sem.sent, n)
+        if codes:
+            out, in_ = out.bitcast(dt.uint8), in_.bitcast(dt.uint8)
+        ids = []
+        for d in dests:
+            rid, pid, _ = topo.addr(d)
+            ids.append(DstId(rid=rid, pnc=pid))
+        g.remote_dma_fused([RemoteDMATransfer(dst_ids=ids, dma_engine_mask=mask, remote_sem=T.sem["a%s%d" % (kind, j)],
+                                              srcs=[in_], dsts=[out for _ in dests])], local_sem=T.sem.sent)
+        sent += bits(mask)
+    if sent:
+        g.wait_ge(T.sem.sent, sent)
 
 
 def rank_program(g, core, T, topo):
     rank = T.rank_of(core)
+    steps = plan(T, topo)
     if rank is None:
-        relay_program(g, core, T, topo)
+        exchange(g, core, T, topo, steps)
         return
     S = T.sem
     near = [d for d in T.cores if d != core and topo.chip(d) == topo.chip(core)]
-    far = far_of(core, T, topo)
-    order = [core] + near + sorted(far, key=lambda c: len(relays(c, T, topo)[0]))
+    far = [d for d in T.cores if topo.chip(d) != topo.chip(core)]
+    order = [core] + near + sorted(far, key=lambda c: not topo.may_write(c, core))
 
     g.sync.dma_start(T.gt[:, 0:EL], T.gr[:, 0:EL]).then_inc(S.lg0, 16)
     g.scalar.dma_start(T.pc[:].bitcast(dt.uint8), T.wc[:]).then_inc(S.lwc, 16)
@@ -165,26 +174,21 @@ def rank_program(g, core, T, topo):
     g.vector.wait_ge(S.lx, 16)
     g.vector.quantize_mx(T.xc[:], T.xs[:], T.xt[:]).then_inc(S.xq, 1)
 
-    sent = made = 0
-    for tiles, dests, mask, what, a, b in calls(core, T, topo):
-        while made < tiles:
-            g.wait_ge(S["vq%d" % made], 1)
-            made += 1
-        sent += send(g, T, topo, rank, dests, mask, what, T["v" + what], a, b)
-    g.wait_ge(S.sent, sent)
+    exchange(g, core, T, topo, steps)
 
+    count = landed(steps, core)
+    g.tensor.wait_ge(S.xq, 1)
     for k, src in enumerate(order):
         j = T.rank_of(src)
-        if src == core:
-            g.tensor.wait_ge(S.xq, 1)
-            for i in range(WT):
-                g.tensor.wait_ge(S["vq%d" % i], 1)
-            cc, cs = T.vc, T.vs
-        else:
-            g.tensor.wait_ge(S["ac%d" % j], arrivals(src, core, "c", T, topo))
-            g.tensor.wait_ge(S["as%d" % j], arrivals(src, core, "s", T, topo))
-            cc, cs = T["rc%d" % j], T["rs%d" % j]
+        cc, cs = (T.vc, T.vs) if src == core else (T["rc%d" % j], T["rs%d" % j])
+        tile0 = "at%d" % j in count
         for i in range(WT):
+            if src == core:
+                g.tensor.wait_ge(S["vq%d" % i], 1)
+            else:
+                for name in ([] if i else ["as%d" % j]) + (["at%d" % j] if tile0 and not i else []) + (
+                        ["ac%d" % j] if i or not tile0 else []):
+                    g.tensor.wait_ge(S[name], count[name])
             q = 2 * k + i
             g.tensor.matmul_mx(T.acc[:, BANK * q:BANK * q + NC], cc[:, TW * i:TW * i + TW], cs[:, TW * i:TW * i + TW],
                                T.xc[:], T.xs[:], True, True).then_inc(S["m%d" % q], 1)

@@ -4,36 +4,40 @@ from concourse.mybir import dt, AluOpType, ActivationFunctionType
 NR = 4
 WT = 2
 NC = 256
+HC = NC // 2
 TW = 128
 EL = 4 * TW
+W = WT * TW
 BANK = 512
+NB = 8
+MID = 3 * TW // 2
 LR = 2.0 ** -4
 
 SCRATCH = {
-    "ramp": ("sbuf", [128, TW], "float32"),
+    "ramp": ("sbuf", [128, TW], "bfloat16"),
     "band": ("sbuf", [128, EL + 4], "bfloat16"),
     "sc": ("sbuf", [128, 4 * TW], "float8_e4m3fn_x4"),
     "ss": ("sbuf", [128, 4 * TW], "uint8"),
-    "pc": ("sbuf", [128, WT * TW], "float8_e4m3fn_x4"),
-    "ps": ("sbuf", [128, WT * TW], "uint8"),
+    "pc": ("sbuf", [128, W], "float8_e4m3fn_x4"),
+    "ps": ("sbuf", [128, W], "uint8"),
     "gt": ("sbuf", [128, WT * EL], "bfloat16"),
     "gs": ("sbuf", [128, WT * EL], "bfloat16"),
     "xt": ("sbuf", [128, 4 * NC], "bfloat16"),
     "xc": ("sbuf", [128, NC], "float8_e4m3fn_x4"),
     "xs": ("sbuf", [128, NC], "uint8"),
     "v": ("sbuf", [128, WT * EL], "bfloat16"),
-    "vc": ("sbuf", [128, WT * TW], "float8_e4m3fn_x4"),
-    "vs": ("sbuf", [128, WT * TW], "uint8"),
+    "vc": ("sbuf", [128, W], "float8_e4m3fn_x4"),
+    "vs": ("sbuf", [128, W], "uint8"),
     "yt": ("sbuf", [128, NR * WT * NC], "float32"),
-    "acc": ("psum", [128, 8 * BANK], "float32"),
+    "acc": ("psum", [128, NB * BANK], "float32"),
 }
 for _j in range(NR):
-    SCRATCH["rc%d" % _j] = ("sbuf", [128, WT * TW], "float8_e4m3fn_x4")
-    SCRATCH["rs%d" % _j] = ("sbuf", [128, WT * TW], "uint8")
+    SCRATCH["rc%d" % _j] = ("sbuf", [128, W], "float8_e4m3fn_x4")
+    SCRATCH["rs%d" % _j] = ("sbuf", [128, W], "uint8")
 
-SEMAPHORES = (["lg0", "lg1", "lwc", "lws", "lx", "ramp", "zero", "ones", "sq", "g0", "g1", "tt0", "tt1", "vq0", "vq1", "xq",
-               "sent", "sty", "stc"]
-              + ["d%d" % k for k in range(8)] + ["m%d" % k for k in range(8)] + ["c%d" % k for k in range(8)]
+SEMAPHORES = (["lg0", "lg1", "lw0", "lw1", "lws", "lx", "ramp", "zero", "ones", "tt0", "tt1", "vq0", "vq1", "xq", "sent", "sty"]
+              + ["q%d" % b for b in range(4)]
+              + ["%s%d" % (w, k) for w in "demnc" for k in range(8)]
               + ["a%s%d" % (w, j) for w in "tcs" for j in range(NR)])
 
 
@@ -42,62 +46,60 @@ def bits(mask):
 
 
 def plan(T, topo):
-    W = WT * TW
     steps, passed = {}, []
 
-    def add(core, needs, j, kind, a, b, dests, mask):
-        steps.setdefault(core, []).append((needs, j, kind, a, b, dests, mask))
+    def add(core, needs, piece, *moves):
+        steps.setdefault(core, []).append((needs,) + piece + (moves,))
 
     for j, src in enumerate(T.cores):
         near = [d for d in T.cores if d != src and topo.chip(d) == topo.chip(src)]
         far = [d for d in T.cores if topo.chip(d) != topo.chip(src)]
         half, full = ["vq0"], ["vq0", "vq1"]
+        tile0, tile1, codes, planes = (j, "t", 0, TW), (j, "c", TW, W), (j, "c", 0, W), (j, "s", 0, W)
+        chipwide = topo.mask(src, near[0])
         if all(topo.may_write(src, d) for d in far):
             off = topo.mask(src, far[0])
-            inner = topo.mask(src, near[0]) & ~off
-            peer = [d for d in far if all(topo.may_write(d, s) for s in near)] or far
-            rest = [d for d in far if d not in peer]
-            add(src, half, j, "t", 0, TW, near, inner)
-            add(src, full, j, "s", 0, W, peer, off)
-            add(src, full, j, "c", 0, W, far, off)
-            add(src, full, j, "c", TW, W, near, inner)
-            add(src, full, j, "s", 0, W, near, inner)
-            if rest:
-                passed.append((peer[0], j, rest, topo.mask(peer[0], rest[0]) & ~topo.mask(peer[0], src)))
+            inner = chipwide & ~off
+            peer = ([d for d in far if all(topo.may_write(d, s) for s in [src] + near)] or far)[0]
+            rest = [d for d in far if d != peer]
+            add(src, half, tile0, (near, inner))
+            add(src, full, planes, ([peer], off), (near, inner))
+            add(src, full, codes, (far, off))
+            add(src, full, tile1, (near, inner))
+            passed.append((peer, ["as%d" % j], planes, (rest, topo.mask(peer, rest[0]) & ~topo.mask(peer, src))))
         else:
             own = [c for c in range(topo.CHIPS * topo.CORES_PER_CHIP)
                    if topo.chip(c) == topo.chip(src) and T.rank_of(c) is None and all(topo.may_write(c, d) for d in far)]
             own.sort(key=lambda c: (topo.die(c) != topo.die(src), c))
             rc, rp = own[:len(far)], own[len(far)]
-            m, nm = topo.mask(src, rc[0]), topo.mask(src, near[0])
-            add(src, half, j, "t", 0, TW, rc, m)
-            add(src, full, j, "s", 0, W, [rp], topo.mask(src, rp))
-            add(src, full, j, "c", TW, W, rc, m)
-            add(src, full, j, "c", 0, W, near, nm)
-            add(src, full, j, "s", 0, W, near, nm)
+            add(src, half, tile0, (rc, chipwide))
+            add(src, full, planes, ([rp] + near, chipwide))
+            add(src, full, tile1, (rc, chipwide))
+            add(src, full, codes, (near, chipwide))
             for r, d in zip(rc, far):
-                add(r, ["at%d" % j], j, "t", 0, TW, [d], topo.mask(r, d))
-                add(r, ["ac%d" % j], j, "c", TW, W, [d], topo.mask(r, d))
-            add(rp, ["as%d" % j], j, "s", 0, W, far, topo.mask(rp, far[0]))
-    for c, j, dests, mask in passed:
-        add(c, ["as%d" % j], j, "s", 0, W, dests, mask)
+                add(r, ["at%d" % j], tile0, ([d], topo.mask(r, d)))
+                add(r, ["ac%d" % j], tile1, ([d], topo.mask(r, d)))
+            add(rp, ["as%d" % j], planes, (far, topo.mask(rp, far[0])))
+    for call in passed:
+        add(*call)
     return steps
 
 
 def landed(steps, dst):
     n = {}
     for own in steps.values():
-        for _, j, kind, _, _, dests, mask in own:
-            if dst in dests:
-                name = "a%s%d" % (kind, j)
-                n[name] = n.get(name, 0) + bits(mask)
+        for _, j, kind, _, _, moves in own:
+            for dests, mask in moves:
+                if dst in dests:
+                    name = "a%s%d" % (kind, j)
+                    n[name] = n.get(name, 0) + bits(mask)
     return n
 
 
 def exchange(g, core, T, topo, steps):
     count = landed(steps, core)
     met, sent = [], 0
-    for needs, j, kind, a, b, dests, mask in steps.get(core, []):
+    for needs, j, kind, a, b, moves in steps.get(core, []):
         for name in needs:
             if name not in met:
                 g.wait_ge(T.sem[name], count.get(name, 1))
@@ -108,13 +110,16 @@ def exchange(g, core, T, topo, steps):
         out, in_ = land[:, a:b], src[:, a:b]
         if codes:
             out, in_ = out.bitcast(dt.uint8), in_.bitcast(dt.uint8)
-        ids = []
-        for d in dests:
-            rid, pid, _ = topo.addr(d)
-            ids.append(DstId(rid=rid, pnc=pid))
-        g.remote_dma_fused([RemoteDMATransfer(dst_ids=ids, dma_engine_mask=mask, remote_sem=T.sem["a%s%d" % (kind, j)],
-                                              srcs=[in_], dsts=[out for _ in dests])], local_sem=T.sem.sent)
-        sent += bits(mask)
+        transfers = []
+        for dests, mask in moves:
+            ids = []
+            for d in dests:
+                rid, pid, _ = topo.addr(d)
+                ids.append(DstId(rid=rid, pnc=pid))
+            transfers.append(RemoteDMATransfer(dst_ids=ids, dma_engine_mask=mask, remote_sem=T.sem["a%s%d" % (kind, j)],
+                                               srcs=[in_], dsts=[out for _ in dests]))
+            sent += bits(mask)
+        g.remote_dma_fused(transfers, local_sem=T.sem.sent)
     if sent:
         g.wait_ge(T.sem.sent, sent)
 
@@ -130,41 +135,50 @@ def rank_program(g, core, T, topo):
     far = [d for d in T.cores if topo.chip(d) != topo.chip(core)]
     order = [core] + near + sorted(far, key=lambda c: not topo.may_write(c, core))
 
-    g.sync.dma_start(T.gt[:, 0:EL], T.gr[:, 0:EL]).then_inc(S.lg0, 16)
-    g.scalar.dma_start(T.pc[:].bitcast(dt.uint8), T.wc[:]).then_inc(S.lwc, 16)
+    g.scalar.dma_start(T.pc[:, 0:TW].bitcast(dt.uint8), T.wc[:, 0:EL]).then_inc(S.lw0, 16)
     g.sync.dma_start(T.ps[:], T.ws[:]).then_inc(S.lws, 16)
-    g.scalar.dma_start(T.gt[:, EL:2 * EL], T.gr[:, EL:2 * EL]).then_inc(S.lg1, 16)
+    g.scalar.dma_start(T.gt[:, 0:EL], T.gr[:, 0:EL]).then_inc(S.lg0, 16)
+    g.sync.wait_ge(S.ramp, 1)
+    g.sync.dma_start(T.pc[:, TW:W].bitcast(dt.uint8), T.wc[:, EL:2 * EL]).then_inc(S.lw1, 16)
+    g.sync.dma_start(T.gt[:, EL:2 * EL], T.gr[:, EL:2 * EL]).then_inc(S.lg1, 16)
+    g.sync.wait_ge(S.lg0, 16)
     g.sync.dma_start(T.xt[:], T.x[:]).then_inc(S.lx, 16)
 
     g.vector.memset(T.band[:], 0.0).then_inc(S.zero, 1)
-    g.iota(T.ramp[:], [[-1, TW]], 3, 4, allow_small_or_imprecise_dtypes=True).then_inc(S.ramp, 1)
+    g.iota(T.ramp[:], [[-1, TW]], 3 - MID, 4, allow_small_or_imprecise_dtypes=True).then_inc(S.ramp, 1)
     g.vector.wait_ge(S.zero, 1)
     g.vector.wait_ge(S.ramp, 1)
     for a in range(4):
         g.vector.tensor_scalar(T.band[32 * a:32 * a + 32, TW * a:TW * a + TW], T.ramp[32 * a:32 * a + 32, :],
-                               float(TW * a), None, AluOpType.is_equal).then_inc(S.ones, 1)
+                               float(TW * a - MID), None, AluOpType.is_equal).then_inc(S.ones, 1)
     g.vector.wait_ge(S.ones, 4)
     for b in range(4):
         g.vector.quantize_mx(T.sc[:, TW * b:TW * b + TW], T.ss[:, TW * b:TW * b + TW],
-                             T.band[:, 3 - b:3 - b + EL]).then_inc(S.sq, 1)
+                             T.band[:, 3 - b:3 - b + EL]).then_inc(S["q%d" % b], 1)
 
-    g.tensor.wait_ge(S.sq, 4)
-    g.tensor.wait_ge(S.lwc, 16)
     g.tensor.wait_ge(S.lws, 16)
     for i in range(WT):
+        g.tensor.wait_ge(S["lw%d" % i], 16)
         for b in range(4):
             k = 4 * i + b
+            if i == 0:
+                g.tensor.wait_ge(S["q%d" % b], 1)
             g.tensor.matmul_mx(T.acc[:, BANK * k:BANK * k + TW], T.sc[:, TW * b:TW * b + TW], T.ss[:, TW * b:TW * b + TW],
                                T.pc[:, TW * i:TW * i + TW], T.ps[:, TW * i:TW * i + TW], True, True).then_inc(S["d%d" % k], 1)
 
-    g.vector.wait_ge(S.lg0, 16)
-    g.vector.tensor_scalar(T.gs[:, 0:EL], T.gt[:, 0:EL], LR, None, AluOpType.mult).then_inc(S.g0, 1)
-    g.scalar.wait_ge(S.lg1, 16)
-    g.scalar.activation(T.gs[:, EL:2 * EL], T.gt[:, EL:2 * EL], ActivationFunctionType.Copy, scale=LR).then_inc(S.g1, 1)
+    for k in range(8):
+        i, b = divmod(k, 4)
+        out, in_ = T.gs[:, EL * i + b:EL * (i + 1):4], T.gt[:, EL * i + b:EL * (i + 1):4]
+        if i == 0 and b % 2 == 0:
+            g.vector.wait_ge(S.lg0, 16)
+            g.vector.tensor_scalar(out, in_, LR, None, AluOpType.mult).then_inc(S["e%d" % k], 1)
+        else:
+            g.scalar.wait_ge(S["lg%d" % i], 16)
+            g.scalar.activation(out, in_, ActivationFunctionType.Copy, scale=LR).then_inc(S["e%d" % k], 1)
     for i in range(WT):
-        g.vector.wait_ge(S["g%d" % i], 1)
         for b in range(4):
             k = 4 * i + b
+            g.vector.wait_ge(S["e%d" % k], 1)
             g.vector.wait_ge(S["d%d" % k], 1)
             g.vector.tensor_tensor(T.v[:, EL * i + b:EL * (i + 1):4], T.acc[:, BANK * k:BANK * k + TW],
                                    T.gs[:, EL * i + b:EL * (i + 1):4], AluOpType.subtract).then_inc(S["tt%d" % i], 1)
@@ -178,33 +192,40 @@ def rank_program(g, core, T, topo):
 
     count = landed(steps, core)
     g.tensor.wait_ge(S.xq, 1)
+    stored = 0
     for k, src in enumerate(order):
         j = T.rank_of(src)
         cc, cs = (T.vc, T.vs) if src == core else (T["rc%d" % j], T["rs%d" % j])
-        tile0 = "at%d" % j in count
-        for i in range(WT):
-            if src == core:
-                g.tensor.wait_ge(S["vq%d" % i], 1)
-            else:
-                for name in ([] if i else ["as%d" % j]) + (["at%d" % j] if tile0 and not i else []) + (
-                        ["ac%d" % j] if i or not tile0 else []):
-                    g.tensor.wait_ge(S[name], count[name])
-            q = 2 * k + i
-            g.tensor.matmul_mx(T.acc[:, BANK * q:BANK * q + NC], cc[:, TW * i:TW * i + TW], cs[:, TW * i:TW * i + TW],
-                               T.xc[:], T.xs[:], True, True).then_inc(S["m%d" % q], 1)
         for i in range(WT):
             q = 2 * k + i
             a = NC * (2 * j + i)
-            out, acc, done = T.yt[:, a:a + NC], T.acc[:, BANK * q:BANK * q + NC], S["c%d" % q]
-            if i == 0:
-                g.vector.wait_ge(S["m%d" % q], 1)
-                g.vector.tensor_copy(out, acc).then_inc(done, 1)
-                dq, st = g.sync, S.sty
+            if src == core:
+                g.tensor.wait_ge(S["vq%d" % i], 1)
             else:
-                g.scalar.wait_ge(S["m%d" % q], 1)
-                g.scalar.activation(out, acc, ActivationFunctionType.Copy).then_inc(done, 1)
-                dq, st = g.scalar, S.stc
-            dq.wait_ge(done, 1)
-            dq.dma_start(T.y[:, a:a + NC], out).then_inc(st, 16)
-    g.sync.wait_ge(S.sty, 16 * NR)
-    g.scalar.wait_ge(S.stc, 16 * NR)
+                alone = "at%d" % j in count
+                for w in ("st" if alone else "sc") if i == 0 else ("c" if alone else ""):
+                    g.tensor.wait_ge(S["a%s%d" % (w, j)], count["a%s%d" % (w, j)])
+            if 2 * q >= NB:
+                g.tensor.wait_ge(S["c%d" % (q - NB // 2)], 2)
+            for h in range(2):
+                p = BANK * ((2 * q + h) % NB)
+                acc, cols = T.acc[:, p:p + HC], slice(HC * h, HC * h + HC)
+                done = S["%s%d" % ("mn"[h], q)]
+                g.tensor.matmul_mx(acc, cc[:, TW * i:TW * i + TW], cs[:, TW * i:TW * i + TW],
+                                   T.xc[:, cols], T.xs[:, cols], True, True).then_inc(done, 1)
+                out = T.yt[:, a + HC * h:a + HC * h + HC]
+                if h == 0:
+                    g.vector.wait_ge(done, 1)
+                    g.vector.tensor_copy(out, acc).then_inc(S["c%d" % q], 1)
+                else:
+                    g.scalar.wait_ge(done, 1)
+                    g.scalar.activation(out, acc, ActivationFunctionType.Copy).then_inc(S["c%d" % q], 1)
+            g.sync.wait_ge(S["c%d" % q], 2)
+            lo, hi = a, a + NC
+            if src == core:
+                if i == 0:
+                    continue
+                lo = a - NC
+            g.sync.dma_start(T.y[:, lo:hi], T.yt[:, lo:hi]).then_inc(S.sty, 16)
+            stored += 16
+    g.sync.wait_ge(S.sty, stored)

from concourse.bass import DstId, RemoteDMATransfer
from concourse.mybir import dt, AluOpType, ActivationFunctionType

NR = 4
WT = 2
NC = 256
HC = NC // 2
TW = 128
EL = 4 * TW
W = WT * TW
BANK = 512
NB = 8
MID = 3 * TW // 2
LR = 2.0 ** -4

SCRATCH = {
    "ramp": ("sbuf", [128, TW], "bfloat16"),
    "band": ("sbuf", [128, EL + 4], "bfloat16"),
    "sc": ("sbuf", [128, 4 * TW], "float8_e4m3fn_x4"),
    "ss": ("sbuf", [128, 4 * TW], "uint8"),
    "pc": ("sbuf", [128, W], "float8_e4m3fn_x4"),
    "ps": ("sbuf", [128, W], "uint8"),
    "gt": ("sbuf", [128, WT * EL], "bfloat16"),
    "gs": ("sbuf", [128, WT * EL], "bfloat16"),
    "xt": ("sbuf", [128, 4 * NC], "bfloat16"),
    "xc": ("sbuf", [128, NC], "float8_e4m3fn_x4"),
    "xs": ("sbuf", [128, NC], "uint8"),
    "v": ("sbuf", [128, WT * EL], "bfloat16"),
    "vc": ("sbuf", [128, W], "float8_e4m3fn_x4"),
    "vs": ("sbuf", [128, W], "uint8"),
    "yt": ("sbuf", [128, NR * WT * NC], "float32"),
    "acc": ("psum", [128, NB * BANK], "float32"),
}
for _j in range(NR):
    SCRATCH["rc%d" % _j] = ("sbuf", [128, W], "float8_e4m3fn_x4")
    SCRATCH["rs%d" % _j] = ("sbuf", [128, W], "uint8")

SEMAPHORES = (["lg0", "lg1", "lw0", "lw1", "lws", "lx", "ramp", "zero", "ones", "tt0", "tt1", "vq0", "vq1", "xq", "sent", "sty"]
              + ["q%d" % b for b in range(4)]
              + ["%s%d" % (w, k) for w in "demnc" for k in range(8)]
              + ["a%s%d" % (w, j) for w in "tcs" for j in range(NR)])


def bits(mask):
    return bin(mask).count("1")


def plan(T, topo):
    steps, passed = {}, []

    def add(core, needs, piece, *moves):
        steps.setdefault(core, []).append((needs,) + piece + (moves,))

    for j, src in enumerate(T.cores):
        near = [d for d in T.cores if d != src and topo.chip(d) == topo.chip(src)]
        far = [d for d in T.cores if topo.chip(d) != topo.chip(src)]
        half, full = ["vq0"], ["vq0", "vq1"]
        tile0, tile1, codes, planes = (j, "t", 0, TW), (j, "c", TW, W), (j, "c", 0, W), (j, "s", 0, W)
        chipwide = topo.mask(src, near[0])
        if all(topo.may_write(src, d) for d in far):
            off = topo.mask(src, far[0])
            inner = chipwide & ~off
            peer = ([d for d in far if all(topo.may_write(d, s) for s in [src] + near)] or far)[0]
            rest = [d for d in far if d != peer]
            add(src, half, tile0, (near, inner))
            add(src, full, planes, ([peer], off), (near, inner))
            add(src, full, codes, (far, off))
            add(src, full, tile1, (near, inner))
            passed.append((peer, ["as%d" % j], planes, (rest, topo.mask(peer, rest[0]) & ~topo.mask(peer, src))))
        else:
            own = [c for c in range(topo.CHIPS * topo.CORES_PER_CHIP)
                   if topo.chip(c) == topo.chip(src) and T.rank_of(c) is None and all(topo.may_write(c, d) for d in far)]
            own.sort(key=lambda c: (topo.die(c) != topo.die(src), c))
            rc, rp = own[:len(far)], own[len(far)]
            add(src, half, tile0, (rc, chipwide))
            add(src, full, planes, ([rp] + near, chipwide))
            add(src, full, tile1, (rc, chipwide))
            add(src, full, codes, (near, chipwide))
            for r, d in zip(rc, far):
                add(r, ["at%d" % j], tile0, ([d], topo.mask(r, d)))
                add(r, ["ac%d" % j], tile1, ([d], topo.mask(r, d)))
            add(rp, ["as%d" % j], planes, (far, topo.mask(rp, far[0])))
    for call in passed:
        add(*call)
    return steps


def landed(steps, dst):
    n = {}
    for own in steps.values():
        for _, j, kind, _, _, moves in own:
            for dests, mask in moves:
                if dst in dests:
                    name = "a%s%d" % (kind, j)
                    n[name] = n.get(name, 0) + bits(mask)
    return n


def exchange(g, core, T, topo, steps):
    count = landed(steps, core)
    met, sent = [], 0
    for needs, j, kind, a, b, moves in steps.get(core, []):
        for name in needs:
            if name not in met:
                g.wait_ge(T.sem[name], count.get(name, 1))
                met.append(name)
        codes = kind != "s"
        land = T["r%s%d" % ("c" if codes else "s", j)]
        src = land if T.rank_of(core) != j else (T.vc if codes else T.vs)
        out, in_ = land[:, a:b], src[:, a:b]
        if codes:
            out, in_ = out.bitcast(dt.uint8), in_.bitcast(dt.uint8)
        transfers = []
        for dests, mask in moves:
            ids = []
            for d in dests:
                rid, pid, _ = topo.addr(d)
                ids.append(DstId(rid=rid, pnc=pid))
            transfers.append(RemoteDMATransfer(dst_ids=ids, dma_engine_mask=mask, remote_sem=T.sem["a%s%d" % (kind, j)],
                                               srcs=[in_], dsts=[out for _ in dests]))
            sent += bits(mask)
        g.remote_dma_fused(transfers, local_sem=T.sem.sent)
    if sent:
        g.wait_ge(T.sem.sent, sent)


def rank_program(g, core, T, topo):
    rank = T.rank_of(core)
    steps = plan(T, topo)
    if rank is None:
        exchange(g, core, T, topo, steps)
        return
    S = T.sem
    near = [d for d in T.cores if d != core and topo.chip(d) == topo.chip(core)]
    far = [d for d in T.cores if topo.chip(d) != topo.chip(core)]
    order = [core] + near + sorted(far, key=lambda c: not topo.may_write(c, core))

    g.scalar.dma_start(T.pc[:, 0:TW].bitcast(dt.uint8), T.wc[:, 0:EL]).then_inc(S.lw0, 16)
    g.sync.dma_start(T.ps[:], T.ws[:]).then_inc(S.lws, 16)
    g.scalar.dma_start(T.gt[:, 0:EL], T.gr[:, 0:EL]).then_inc(S.lg0, 16)
    g.sync.wait_ge(S.ramp, 1)
    g.sync.dma_start(T.pc[:, TW:W].bitcast(dt.uint8), T.wc[:, EL:2 * EL]).then_inc(S.lw1, 16)
    g.sync.dma_start(T.gt[:, EL:2 * EL], T.gr[:, EL:2 * EL]).then_inc(S.lg1, 16)
    g.sync.wait_ge(S.lg0, 16)
    g.sync.dma_start(T.xt[:], T.x[:]).then_inc(S.lx, 16)

    g.vector.memset(T.band[:], 0.0).then_inc(S.zero, 1)
    g.iota(T.ramp[:], [[-1, TW]], 3 - MID, 4, allow_small_or_imprecise_dtypes=True).then_inc(S.ramp, 1)
    g.vector.wait_ge(S.zero, 1)
    g.vector.wait_ge(S.ramp, 1)
    for a in range(4):
        g.vector.tensor_scalar(T.band[32 * a:32 * a + 32, TW * a:TW * a + TW], T.ramp[32 * a:32 * a + 32, :],
                               float(TW * a - MID), None, AluOpType.is_equal).then_inc(S.ones, 1)
    g.vector.wait_ge(S.ones, 4)
    for b in range(4):
        g.vector.quantize_mx(T.sc[:, TW * b:TW * b + TW], T.ss[:, TW * b:TW * b + TW],
                             T.band[:, 3 - b:3 - b + EL]).then_inc(S["q%d" % b], 1)

    g.tensor.wait_ge(S.lws, 16)
    for i in range(WT):
        g.tensor.wait_ge(S["lw%d" % i], 16)
        for b in range(4):
            k = 4 * i + b
            if i == 0:
                g.tensor.wait_ge(S["q%d" % b], 1)
            g.tensor.matmul_mx(T.acc[:, BANK * k:BANK * k + TW], T.sc[:, TW * b:TW * b + TW], T.ss[:, TW * b:TW * b + TW],
                               T.pc[:, TW * i:TW * i + TW], T.ps[:, TW * i:TW * i + TW], True, True).then_inc(S["d%d" % k], 1)

    for k in range(8):
        i, b = divmod(k, 4)
        out, in_ = T.gs[:, EL * i + b:EL * (i + 1):4], T.gt[:, EL * i + b:EL * (i + 1):4]
        if i == 0 and b % 2 == 0:
            g.vector.wait_ge(S.lg0, 16)
            g.vector.tensor_scalar(out, in_, LR, None, AluOpType.mult).then_inc(S["e%d" % k], 1)
        else:
            g.scalar.wait_ge(S["lg%d" % i], 16)
            g.scalar.activation(out, in_, ActivationFunctionType.Copy, scale=LR).then_inc(S["e%d" % k], 1)
    for i in range(WT):
        for b in range(4):
            k = 4 * i + b
            g.vector.wait_ge(S["e%d" % k], 1)
            g.vector.wait_ge(S["d%d" % k], 1)
            g.vector.tensor_tensor(T.v[:, EL * i + b:EL * (i + 1):4], T.acc[:, BANK * k:BANK * k + TW],
                                   T.gs[:, EL * i + b:EL * (i + 1):4], AluOpType.subtract).then_inc(S["tt%d" % i], 1)
        g.vector.wait_ge(S["tt%d" % i], 4)
        g.vector.quantize_mx(T.vc[:, TW * i:TW * i + TW], T.vs[:, TW * i:TW * i + TW],
                             T.v[:, EL * i:EL * i + EL]).then_inc(S["vq%d" % i], 1)
    g.vector.wait_ge(S.lx, 16)
    g.vector.quantize_mx(T.xc[:], T.xs[:], T.xt[:]).then_inc(S.xq, 1)

    exchange(g, core, T, topo, steps)

    count = landed(steps, core)
    g.tensor.wait_ge(S.xq, 1)
    stored = 0
    for k, src in enumerate(order):
        j = T.rank_of(src)
        cc, cs = (T.vc, T.vs) if src == core else (T["rc%d" % j], T["rs%d" % j])
        for i in range(WT):
            q = 2 * k + i
            a = NC * (2 * j + i)
            if src == core:
                g.tensor.wait_ge(S["vq%d" % i], 1)
            else:
                alone = "at%d" % j in count
                for w in ("st" if alone else "sc") if i == 0 else ("c" if alone else ""):
                    g.tensor.wait_ge(S["a%s%d" % (w, j)], count["a%s%d" % (w, j)])
            if 2 * q >= NB:
                g.tensor.wait_ge(S["c%d" % (q - NB // 2)], 2)
            for h in range(2):
                p = BANK * ((2 * q + h) % NB)
                acc, cols = T.acc[:, p:p + HC], slice(HC * h, HC * h + HC)
                done = S["%s%d" % ("mn"[h], q)]
                g.tensor.matmul_mx(acc, cc[:, TW * i:TW * i + TW], cs[:, TW * i:TW * i + TW],
                                   T.xc[:, cols], T.xs[:, cols], True, True).then_inc(done, 1)
                out = T.yt[:, a + HC * h:a + HC * h + HC]
                if h == 0:
                    g.vector.wait_ge(done, 1)
                    g.vector.tensor_copy(out, acc).then_inc(S["c%d" % q], 1)
                else:
                    g.scalar.wait_ge(done, 1)
                    g.scalar.activation(out, acc, ActivationFunctionType.Copy).then_inc(S["c%d" % q], 1)
            g.sync.wait_ge(S["c%d" % q], 2)
            lo, hi = a, a + NC
            if src == core:
                if i == 0:
                    continue
                lo = a - NC
            g.sync.dma_start(T.y[:, lo:hi], T.yt[:, lo:hi]).then_inc(S.sty, 16)
            stored += 16
    g.sync.wait_ge(S.sty, stored)
